import numpy as np
import ml_dtypes


def mxq(x, axis, fmt="e4m3"):
    dtype, down = {"e4m3": (ml_dtypes.float8_e4m3fn, 7), "e5m2": (ml_dtypes.float8_e5m2, 14)}[fmt]
    v = np.moveaxis(np.asarray(x, np.float32).astype(ml_dtypes.bfloat16).astype(np.float64), axis, -1)
    blocks = v.reshape(v.shape[:-1] + (-1, 32))
    amax = np.abs(blocks).max(-1, keepdims=True)
    byte = np.maximum(np.where(amax > 0, np.frexp(amax)[1] - 1 + 127, 0) - down, 1)
    scale = np.exp2(byte - 127.0)
    codes = (blocks / scale).astype(np.float32).astype(dtype).astype(np.float64)
    return np.moveaxis((codes * scale).reshape(v.shape), -1, axis)


WIDE = False


def mx_kscale(k):
    if not WIDE:
        return np.ones(k)
    levels = np.array([10, -10, 5, -5, 0])
    if k % 512:
        return np.exp2(np.random.permutation(np.resize(levels, k // 32))).repeat(32)
    a = np.empty((k // 512, 16))
    for p in range(k // 512):
        a[p, :8] = np.random.permutation(np.resize(levels, 8))
        for g in range(8):
            far = levels[np.abs(levels - a[p, g]) >= 10]
            a[p, g + 8] = far[np.random.randint(len(far))]
    return np.exp2(a.ravel()).repeat(32)


def f64(x):
    return np.asarray(x).astype(np.float64)


def striped(idx):
    return np.tile(np.asarray(idx).reshape(-1, 16).T, (8, 1)).astype(np.uint16)


def unstriped(offs):
    return offs[:16].T.reshape(-1).astype(np.int64)


E2M1 = np.array([0.0, 0.5, 1.0, 1.5, 2.0, 3.0, 4.0, 6.0, -0.0, -0.5, -1.0, -1.5, -2.0, -3.0, -4.0, -6.0])


def pack_weight(w, fmt):
    k, n = w.shape
    w = f64(np.asarray(w, np.float32).astype(ml_dtypes.bfloat16)).reshape(k // 32, 32, n)
    amax = np.abs(w).max(1)
    if fmt == "e4m3":
        byte = np.frexp(amax)[1] - 1 + 127 - 7
    else:
        mant, ex = np.frexp(amax / 6.0)
        byte = np.where(mant > 0.5, ex, ex - 1) + 127
    byte = np.clip(np.where(amax > 0, byte, 1), 1, 254)
    scaled = (w * np.exp2(127.0 - byte)[:, None, :]).reshape(k, n).astype(np.float32)
    by_word = np.ascontiguousarray(scaled.reshape(k // 512, 128, 4, n).transpose(0, 1, 3, 2))
    if fmt == "e4m3":
        words = by_word.astype(ml_dtypes.float8_e4m3fn).view(np.uint8)
    else:
        c = by_word.astype(ml_dtypes.float4_e2m1fn).view(np.uint8) & 0xF
        words = (c[..., 0::2] | (c[..., 1::2] << 4)).reshape(k // 512, 128, 2 * n)
    return np.ascontiguousarray(words), np.ascontiguousarray(byte.astype(np.uint8).reshape(k // 512, 16, n))


def unpack_weight(words, scales, fmt):
    g, _, n = scales.shape
    words = np.ascontiguousarray(words).reshape(g, 128, n, -1)
    if fmt == "e4m3":
        vals = words.view(ml_dtypes.float8_e4m3fn).astype(np.float64)
    else:
        nib = np.empty((g, 128, n, 4), np.uint8)
        nib[..., 0::2] = words & 0xF
        nib[..., 1::2] = words >> 4
        vals = E2M1[nib]
    vals = vals * np.repeat(np.exp2(scales.astype(np.float64) - 127.0), 8, axis=1)[..., None]
    return vals.transpose(0, 1, 3, 2).reshape(g * 512, n)


D, T, U, I, J, G = 512, 1024, 1024, 256, 512, 32


def setup_inputs():
    n = np.random.standard_normal
    idx = np.random.permutation(T)[:I]
    idx2 = np.random.permutation(U)[:J]
    fd = mx_kscale(D)
    tabbp = pack_weight(n((D, U)) / fd[:, None], "e4m3")
    return {
        "taba": (n((D, T)) * 1 / np.sqrt(D) * fd[:, None]).astype(np.float32),
        "tabb_words": tabbp[0],
        "tabb_scales": tabbp[1],
        "aim": (np.random.uniform(0.3, 2.0, (I, G))).astype(np.float32),
        "old": (0.3 * n((I, J))).astype(np.float32),
        "offs": striped(idx),
        "offs2": striped(idx2),
    }


def reference(taba, tabb_words, tabb_scales, aim, old, offs, offs2):
    idx = unstriped(offs)
    idx2 = unstriped(offs2)
    tabbu = unpack_weight(tabb_words, tabb_scales, "e4m3")
    tabaidxq = mxq(f64(taba)[:, idx], 0, "e4m3")
    tabbidx2g = tabbu[:, idx2]
    s = tabaidxq.T @ tabbidx2g
    v1 = np.sqrt(np.square(s).reshape(I, G, J // G).mean(axis=2) + 0.05)
    dv1 = (v1 - f64(aim)) * 2.0
    e1 = dv1 * 0.5 / np.sqrt(np.square(s).reshape(I, G, J // G).mean(axis=2) + 0.05) / 16.0
    r1 = np.repeat(e1, J // G, axis=1)
    ds = r1 * s * 2.0
    y = ds * 8.0 + f64(old)
    return y

@@ -1,0 +1,121 @@
+from contextlib import ExitStack
+
+import concourse.mybir as mybir
+
+D, T, U, I, J, G = 512, 1024, 1024, 256, 512, 32
+FLOPS = 2 * D * I * J
+
+F32 = mybir.dt.float32
+BF16 = mybir.dt.bfloat16
+I32 = mybir.dt.int32
+U32 = mybir.dt.uint32
+U16 = mybir.dt.uint16
+U8 = mybir.dt.uint8
+FP8X4 = mybir.dt.float8_e4m3fn_x4
+ACT = mybir.ActivationFunctionType
+ALU = mybir.AluOpType
+AX = mybir.AxisListType
+
+P = 128
+PACK = 4
+GROUP = J // G
+ROW_TILES = I // P
+CHUNK = 128
+CHUNKS = J // CHUNK
+CG = CHUNK // GROUP
+
+
+def tile_attend_bgroupspread_kernel(tc, taba, tabb_words, tabb_scales, aim, old, offs, offs2, out):
+    nc = tc.nc
+    with ExitStack() as ctx:
+        keep = ctx.enter_context(tc.tile_pool(name="keep", bufs=1))
+        psum = ctx.enter_context(tc.psum_pool(name="psum", bufs=1))
+
+        list_b = keep.tile([P, J // 16], U16, name="list_b")
+        list_a = keep.tile([P, I // 16], U16, name="list_a")
+        nc.sync.dma_start(list_b[:], offs2)
+        nc.sync.dma_start(list_a[:], offs)
+
+        scale_table = keep.tile([P, U], U8, name="scale_table", align_bytes=64)
+        nc.vector.memset(scale_table[0:112, :].bitcast(I32), 0)
+        one = keep.tile([P, 1], F32, name="one")
+        warm = keep.tile([P, 1], F32, name="warm")
+        nc.scalar.dma_start(scale_table[112:128, :].bitcast(I32), tabb_scales[0].bitcast(I32))
+        b_scales = keep.tile([P, J], U8, name="b_scales", align_bytes=64)
+        nc.vector.memset(b_scales[:].bitcast(I32), 0)
+        nc.vector.memset(one[:], 1.0)
+        nc.scalar.activation(warm[:], one[:], ACT.Abs_reciprocal_sqrt)
+
+        planes_hbm = taba.rearrange("(p t) c -> t p c", t=PACK)
+        planes = []
+        for t in range(PACK):
+            plane = keep.tile([P, T], F32, name="plane%d" % t, tag="plane%d" % t, align_bytes=64)
+            nc.sync.dma_start(plane[:], planes_hbm[t])
+            planes.append(plane)
+        word_table = keep.tile([P, U], U32, name="word_table", align_bytes=64)
+        nc.sync.dma_start(word_table[:].bitcast(I32),
+                          tabb_words[0].rearrange("p n t -> p (n t)").bitcast(I32))
+        aim_sb = keep.tile([P, ROW_TILES, G], F32, name="aim_sb")
+        nc.gpsimd.dma_start(aim_sb[:], aim.rearrange("(t p) g -> p t g", p=P))
+
+        picked_scales = keep.tile([P, J], U8, name="picked_scales", align_bytes=64)
+        nc.vector.tensor_copy(picked_scales[:], scale_table[:].indirect(list_b[:]))
+        for q in range(4):
+            nc.scalar.dma_start(b_scales[32 * q:32 * q + 4, :].bitcast(I32),
+                                picked_scales[112 + 4 * q:112 + 4 * q + 4, :].bitcast(I32))
+
+        grouped = keep.tile([P, I, PACK], BF16, name="grouped", align_bytes=64)
+        for t in range(PACK - 1):
+            nc.vector.tensor_copy(grouped[:, :, t], planes[t][:].indirect(list_a[:]))
+        old_sb = keep.tile([P, ROW_TILES, J], F32, name="old_sb", tag="plane0", align_bytes=64)
+        nc.sync.dma_start(old_sb[:], old.rearrange("(t p) j -> p t j", p=P))
+        for r in range(ROW_TILES):
+            nc.vector.tensor_copy(grouped[:, r * P:(r + 1) * P, PACK - 1],
+                                  planes[PACK - 1][:].indirect(list_a[:, 8 * r:8 * r + 8]))
+        a_codes, a_scales = [], []
+        for r in range(ROW_TILES):
+            codes = keep.tile([P, P], U32, name="a_codes%d" % r, align_bytes=64)
+            scales = keep.tile([P, P], U8, name="a_scales%d" % r, align_bytes=64)
+            nc.vector.quantize_mx(out=codes[:].bitcast(FP8X4), scales=scales[:],
+                                  in_=grouped[:, r * P:(r + 1) * P, :].rearrange("p c t -> p (c t)"))
+            a_codes.append(codes)
+            a_scales.append(scales)
+
+        out_v = out.rearrange("(t p) j -> p t j", p=P)
+        scores, squares, sums, inv, ratio, scaled = [], [], [], [], [], []
+        for c in range(CHUNKS):
+            cols = slice(c * CHUNK, (c + 1) * CHUNK)
+            b_words = keep.tile([P, CHUNK], U32, name="b_words%d" % c, align_bytes=64)
+            nc.vector.tensor_copy(b_words[:], word_table[:].indirect(list_b[:, c * 8:(c + 1) * 8]))
+            bank = psum.tile([P, ROW_TILES, CHUNK], F32, name="bank%d" % c)
+            for r in range(ROW_TILES):
+                nc.tensor.matmul_mx(out=bank[:, r, :], lhsT=a_codes[r][:].bitcast(FP8X4), lhsT_scale=a_scales[r][:],
+                                    rhs=b_words[:].bitcast(FP8X4), rhs_scale=b_scales[:, cols],
+                                    start=True, stop=True)
+            scores.append(bank)
+            sq = keep.tile([P, ROW_TILES * CHUNK], F32, name="sq%d" % c)
+            nc.scalar.activation(sq[:], bank[:].rearrange("p t j -> p (t j)"), ACT.Square)
+            squares.append(sq)
+        for c in range(CHUNKS):
+            sm = keep.tile([P, ROW_TILES * CG], F32, name="sum%d" % c)
+            nc.vector.tensor_reduce(sm[:], squares[c][:].rearrange("p (g e) -> p g e", e=GROUP), AX.X, ALU.add)
+            rs = keep.tile([P, ROW_TILES * CG], F32, name="inv%d" % c)
+            nc.scalar.activation(rs[:], sm[:], ACT.Abs_reciprocal_sqrt, bias=0.05, scale=1.0 / GROUP)
+            inv.append(rs)
+        for c in range(CHUNKS):
+            qt = keep.tile([P, ROW_TILES, CG], F32, name="ratio%d" % c)
+            nc.vector.tensor_tensor(qt[:], inv[c][:].rearrange("p (t g) -> p t g", g=CG),
+                                    aim_sb[:, :, c * CG:(c + 1) * CG], ALU.mult)
+            ratio.append(qt)
+        for c in range(CHUNKS):
+            cols = slice(c * CHUNK, (c + 1) * CHUNK)
+            sc = keep.tile([P, ROW_TILES, CHUNK], F32, name="scaled%d" % c)
+            nc.vector.scalar_tensor_tensor(
+                sc[:].rearrange("p t (g e) -> p (t g) e", e=GROUP),
+                ratio[c][:].rearrange("p t g -> p (t g)").unsqueeze(2).to_broadcast([P, ROW_TILES * CG, GROUP]),
+                1.0,
+                scores[c][:].rearrange("p t (g e) -> p (t g) e", e=GROUP),
+                ALU.subtract, ALU.mult)
+            res = keep.tile([P, ROW_TILES, CHUNK], F32, name="res%d" % c)
+            nc.vector.tensor_tensor(res[:], old_sb[:, :, cols], sc[:], ALU.subtract)
+            nc.sync.dma_start(out_v[:, :, cols], res[:])

@@ -23,6 +23,8 @@ ROW_TILES = I // P
 CHUNK = 128
 CHUNKS = J // CHUNK
 CG = CHUNK // GROUP
+SCALE_ROWS = 16
+SCALE_BASE = P - SCALE_ROWS
 
 
 def tile_attend_bgroupspread_kernel(tc, taba, tabb_words, tabb_scales, aim, old, offs, offs2, out):
@@ -31,47 +33,47 @@ def tile_attend_bgroupspread_kernel(tc, taba, tabb_words, tabb_scales, aim, old,
         keep = ctx.enter_context(tc.tile_pool(name="keep", bufs=1))
         psum = ctx.enter_context(tc.psum_pool(name="psum", bufs=1))
 
-        list_b = keep.tile([P, J // 16], U16, name="list_b")
-        list_a = keep.tile([P, I // 16], U16, name="list_a")
-        nc.sync.dma_start(list_b[:], offs2)
-        nc.sync.dma_start(list_a[:], offs)
-
-        scale_table = keep.tile([P, U], U8, name="scale_table", align_bytes=64)
-        nc.vector.memset(scale_table[0:112, :].bitcast(I32), 0)
-        one = keep.tile([P, 1], F32, name="one")
-        warm = keep.tile([P, 1], F32, name="warm")
-        nc.scalar.dma_start(scale_table[112:128, :].bitcast(I32), tabb_scales[0].bitcast(I32))
-        b_scales = keep.tile([P, J], U8, name="b_scales", align_bytes=64)
-        nc.vector.memset(b_scales[:].bitcast(I32), 0)
-        nc.vector.memset(one[:], 1.0)
-        nc.scalar.activation(warm[:], one[:], ACT.Abs_reciprocal_sqrt)
-
         planes_hbm = taba.rearrange("(p t) c -> t p c", t=PACK)
         planes = []
         for t in range(PACK):
             plane = keep.tile([P, T], F32, name="plane%d" % t, tag="plane%d" % t, align_bytes=64)
-            nc.sync.dma_start(plane[:], planes_hbm[t])
+            nc.scalar.dma_start(plane[:], planes_hbm[t])
             planes.append(plane)
         word_table = keep.tile([P, U], U32, name="word_table", align_bytes=64)
-        nc.sync.dma_start(word_table[:].bitcast(I32),
-                          tabb_words[0].rearrange("p n t -> p (n t)").bitcast(I32))
-        aim_sb = keep.tile([P, ROW_TILES, G], F32, name="aim_sb")
-        nc.gpsimd.dma_start(aim_sb[:], aim.rearrange("(t p) g -> p t g", p=P))
+        nc.scalar.dma_start(word_table[:].bitcast(I32),
+                            tabb_words[0].rearrange("p n t -> p (n t)").bitcast(I32))
+
+        list_b = keep.tile([P, J // 16], U16, name="list_b")
+        list_a = keep.tile([P, I // 16], U16, name="list_a")
+        scale_table = keep.tile([P, U], U8, name="scale_table", align_bytes=64)
+        nc.sync.dma_start(list_b[:], offs2)
+        nc.sync.dma_start(scale_table[SCALE_BASE:P, :].bitcast(I32), tabb_scales[0].bitcast(I32))
+        nc.sync.dma_start(list_a[:], offs)
+
+        nc.vector.memset(scale_table[0:SCALE_BASE, :].bitcast(I32), 0)
+        b_scales = keep.tile([P, J], U8, name="b_scales", align_bytes=64)
+        nc.vector.memset(b_scales[:].bitcast(I32), 0)
+        one = keep.tile([P, 1], F32, name="one")
+        warm = keep.tile([P, 1], F32, name="warm")
+        nc.vector.memset(one[:], 1.0)
+        nc.scalar.activation(warm[:], one[:], ACT.Abs_reciprocal_sqrt)
 
         picked_scales = keep.tile([P, J], U8, name="picked_scales", align_bytes=64)
         nc.vector.tensor_copy(picked_scales[:], scale_table[:].indirect(list_b[:]))
         for q in range(4):
-            nc.scalar.dma_start(b_scales[32 * q:32 * q + 4, :].bitcast(I32),
-                                picked_scales[112 + 4 * q:112 + 4 * q + 4, :].bitcast(I32))
+            nc.sync.dma_start(b_scales[32 * q:32 * q + 4, :].bitcast(I32),
+                              picked_scales[SCALE_BASE + 4 * q:SCALE_BASE + 4 * q + 4, :].bitcast(I32))
 
         grouped = keep.tile([P, I, PACK], BF16, name="grouped", align_bytes=64)
         for t in range(PACK - 1):
             nc.vector.tensor_copy(grouped[:, :, t], planes[t][:].indirect(list_a[:]))
-        old_sb = keep.tile([P, ROW_TILES, J], F32, name="old_sb", tag="plane0", align_bytes=64)
-        nc.sync.dma_start(old_sb[:], old.rearrange("(t p) j -> p t j", p=P))
+        aim_sb = keep.tile([P, ROW_TILES, G], F32, name="aim_sb", tag="plane2", align_bytes=64)
+        nc.sync.dma_start(aim_sb[:], aim.rearrange("(t p) g -> p t g", p=P))
         for r in range(ROW_TILES):
             nc.vector.tensor_copy(grouped[:, r * P:(r + 1) * P, PACK - 1],
                                   planes[PACK - 1][:].indirect(list_a[:, 8 * r:8 * r + 8]))
+        old_sb = keep.tile([P, ROW_TILES, J], F32, name="old_sb", tag="plane3", align_bytes=64)
+        nc.sync.dma_start(old_sb[:], old.rearrange("(t p) j -> p t j", p=P))
         a_codes, a_scales = [], []
         for r in range(ROW_TILES):
             codes = keep.tile([P, P], U32, name="a_codes%d" % r, align_bytes=64)
@@ -82,40 +84,60 @@ def tile_attend_bgroupspread_kernel(tc, taba, tabb_words, tabb_scales, aim, old,
             a_scales.append(scales)
 
         out_v = out.rearrange("(t p) j -> p t j", p=P)
-        scores, squares, sums, inv, ratio, scaled = [], [], [], [], [], []
+        b_words = []
         for c in range(CHUNKS):
+            picked = keep.tile([P, CHUNK], U32, name="b_words%d" % c, align_bytes=64)
+            nc.vector.tensor_copy(picked[:], word_table[:].indirect(list_b[:, c * 8:(c + 1) * 8]))
+            b_words.append(picked)
+
+        pieces, squares, inv, ratio, scaled = {}, {}, {}, {}, {}
+
+        def score(c):
             cols = slice(c * CHUNK, (c + 1) * CHUNK)
-            b_words = keep.tile([P, CHUNK], U32, name="b_words%d" % c, align_bytes=64)
-            nc.vector.tensor_copy(b_words[:], word_table[:].indirect(list_b[:, c * 8:(c + 1) * 8]))
-            bank = psum.tile([P, ROW_TILES, CHUNK], F32, name="bank%d" % c)
-            for r in range(ROW_TILES):
-                nc.tensor.matmul_mx(out=bank[:, r, :], lhsT=a_codes[r][:].bitcast(FP8X4), lhsT_scale=a_scales[r][:],
-                                    rhs=b_words[:].bitcast(FP8X4), rhs_scale=b_scales[:, cols],
-                                    start=True, stop=True)
-            scores.append(bank)
-            sq = keep.tile([P, ROW_TILES * CHUNK], F32, name="sq%d" % c)
-            nc.scalar.activation(sq[:], bank[:].rearrange("p t j -> p (t j)"), ACT.Square)
-            squares.append(sq)
-        for c in range(CHUNKS):
+            per_bank = 1 if c < 1 else ROW_TILES
+            pieces[c], squares[c] = [], []
+            for r0 in range(0, ROW_TILES, per_bank):
+                bank = psum.tile([P, per_bank, CHUNK], F32, name="bank%d_%d" % (c, r0))
+                for r in range(r0, r0 + per_bank):
+                    nc.tensor.matmul_mx(out=bank[:, r - r0, :], lhsT=a_codes[r][:].bitcast(FP8X4),
+                                        lhsT_scale=a_scales[r][:], rhs=b_words[c][:].bitcast(FP8X4),
+                                        rhs_scale=b_scales[:, cols], start=True, stop=True)
+                sq = keep.tile([P, per_bank * CHUNK], F32, name="sq%d_%d" % (c, r0))
+                nc.scalar.activation(sq[:], bank[:].rearrange("p t j -> p (t j)"), ACT.Square)
+                pieces[c].append((bank, r0, per_bank))
+                squares[c].append(sq)
+
+        def spread(c):
             sm = keep.tile([P, ROW_TILES * CG], F32, name="sum%d" % c)
-            nc.vector.tensor_reduce(sm[:], squares[c][:].rearrange("p (g e) -> p g e", e=GROUP), AX.X, ALU.add)
-            rs = keep.tile([P, ROW_TILES * CG], F32, name="inv%d" % c)
-            nc.scalar.activation(rs[:], sm[:], ACT.Abs_reciprocal_sqrt, bias=0.05, scale=1.0 / GROUP)
-            inv.append(rs)
-        for c in range(CHUNKS):
-            qt = keep.tile([P, ROW_TILES, CG], F32, name="ratio%d" % c)
-            nc.vector.tensor_tensor(qt[:], inv[c][:].rearrange("p (t g) -> p t g", g=CG),
+            for (bank, r0, n), sq in zip(pieces[c], squares[c]):
+                nc.vector.tensor_reduce(sm[:, r0 * CG:(r0 + n) * CG],
+                                        sq[:].rearrange("p (g e) -> p g e", e=GROUP), AX.X, ALU.add)
+            inv[c] = keep.tile([P, ROW_TILES * CG], F32, name="inv%d" % c)
+            nc.scalar.activation(inv[c][:], sm[:], ACT.Abs_reciprocal_sqrt, bias=0.05, scale=1.0 / GROUP)
+
+        def make_ratio(c):
+            ratio[c] = keep.tile([P, ROW_TILES, CG], F32, name="ratio%d" % c)
+            nc.vector.tensor_tensor(ratio[c][:], inv[c][:].rearrange("p (t g) -> p t g", g=CG),
                                     aim_sb[:, :, c * CG:(c + 1) * CG], ALU.mult)
-            ratio.append(qt)
-        for c in range(CHUNKS):
+
+        def scale_scores(c):
+            scaled[c] = keep.tile([P, ROW_TILES, CHUNK], F32, name="scaled%d" % c)
+            for bank, r0, n in pieces[c]:
+                nc.vector.scalar_tensor_tensor(
+                    scaled[c][:, r0:r0 + n, :].rearrange("p t (g e) -> p (t g) e", e=GROUP),
+                    ratio[c][:, r0:r0 + n, :].rearrange("p t g -> p (t g)").unsqueeze(2).to_broadcast([P, n * CG, GROUP]),
+                    1.0,
+                    bank[:].rearrange("p t (g e) -> p (t g) e", e=GROUP),
+                    ALU.subtract, ALU.mult)
+
+        def finish(c):
             cols = slice(c * CHUNK, (c + 1) * CHUNK)
-            sc = keep.tile([P, ROW_TILES, CHUNK], F32, name="scaled%d" % c)
-            nc.vector.scalar_tensor_tensor(
-                sc[:].rearrange("p t (g e) -> p (t g) e", e=GROUP),
-                ratio[c][:].rearrange("p t g -> p (t g)").unsqueeze(2).to_broadcast([P, ROW_TILES * CG, GROUP]),
-                1.0,
-                scores[c][:].rearrange("p t (g e) -> p (t g) e", e=GROUP),
-                ALU.subtract, ALU.mult)
             res = keep.tile([P, ROW_TILES, CHUNK], F32, name="res%d" % c)
-            nc.vector.tensor_tensor(res[:], old_sb[:, :, cols], sc[:], ALU.subtract)
+            nc.vector.tensor_tensor(res[:], old_sb[:, :, cols], scaled[c][:], ALU.subtract)
             nc.sync.dma_start(out_v[:, :, cols], res[:])
+
+        stages = (finish, scale_scores, make_ratio, spread, score)
+        for step in range(CHUNKS + len(stages) - 1):
+            for lag, stage in enumerate(reversed(stages)):
+                if 0 <= step - lag < CHUNKS:
+                    stage(step - lag)

@@ -33,22 +33,18 @@ def tile_attend_bgroupspread_kernel(tc, taba, tabb_words, tabb_scales, aim, old,
         keep = ctx.enter_context(tc.tile_pool(name="keep", bufs=1))
         psum = ctx.enter_context(tc.psum_pool(name="psum", bufs=1))
 
+        list_b = keep.tile([P, J // 16], U16, name="list_b")
+        list_a = keep.tile([P, I // 16], U16, name="list_a")
+        nc.sync.dma_start(list_b[:], offs2)
+        scale_table = keep.tile([P, U], U8, name="scale_table", align_bytes=64)
+        nc.scalar.dma_start(scale_table[SCALE_BASE:P, :].bitcast(I32), tabb_scales[0].bitcast(I32))
+        nc.sync.dma_start(list_a[:], offs)
         planes_hbm = taba.rearrange("(p t) c -> t p c", t=PACK)
         planes = []
         for t in range(PACK):
             plane = keep.tile([P, T], F32, name="plane%d" % t, tag="plane%d" % t, align_bytes=64)
             nc.scalar.dma_start(plane[:], planes_hbm[t])
             planes.append(plane)
-        word_table = keep.tile([P, U], U32, name="word_table", align_bytes=64)
-        nc.scalar.dma_start(word_table[:].bitcast(I32),
-                            tabb_words[0].rearrange("p n t -> p (n t)").bitcast(I32))
-
-        list_b = keep.tile([P, J // 16], U16, name="list_b")
-        list_a = keep.tile([P, I // 16], U16, name="list_a")
-        scale_table = keep.tile([P, U], U8, name="scale_table", align_bytes=64)
-        nc.sync.dma_start(list_b[:], offs2)
-        nc.sync.dma_start(scale_table[SCALE_BASE:P, :].bitcast(I32), tabb_scales[0].bitcast(I32))
-        nc.sync.dma_start(list_a[:], offs)
 
         nc.vector.memset(scale_table[0:SCALE_BASE, :].bitcast(I32), 0)
         b_scales = keep.tile([P, J], U8, name="b_scales", align_bytes=64)
@@ -60,13 +56,16 @@ def tile_attend_bgroupspread_kernel(tc, taba, tabb_words, tabb_scales, aim, old,
 
         picked_scales = keep.tile([P, J], U8, name="picked_scales", align_bytes=64)
         nc.vector.tensor_copy(picked_scales[:], scale_table[:].indirect(list_b[:]))
-        for q in range(4):
-            nc.sync.dma_start(b_scales[32 * q:32 * q + 4, :].bitcast(I32),
+        for q, queue in enumerate((nc.gpsimd, nc.scalar, nc.scalar, nc.scalar)):
+            queue.dma_start(b_scales[32 * q:32 * q + 4, :].bitcast(I32),
                               picked_scales[SCALE_BASE + 4 * q:SCALE_BASE + 4 * q + 4, :].bitcast(I32))
 
         grouped = keep.tile([P, I, PACK], BF16, name="grouped", align_bytes=64)
         for t in range(PACK - 1):
             nc.vector.tensor_copy(grouped[:, :, t], planes[t][:].indirect(list_a[:]))
+        word_table = keep.tile([P, U], U32, name="word_table", tag="plane0", align_bytes=64)
+        nc.scalar.dma_start(word_table[:].bitcast(I32),
+                            tabb_words[0].rearrange("p n t -> p (n t)").bitcast(I32))
         aim_sb = keep.tile([P, ROW_TILES, G], F32, name="aim_sb", tag="plane2", align_bytes=64)
         nc.sync.dma_start(aim_sb[:], aim.rearrange("(t p) g -> p t g", p=P))
         for r in range(ROW_TILES):
@@ -133,8 +132,13 @@ def tile_attend_bgroupspread_kernel(tc, taba, tabb_words, tabb_scales, aim, old,
         def finish(c):
             cols = slice(c * CHUNK, (c + 1) * CHUNK)
             res = keep.tile([P, ROW_TILES, CHUNK], F32, name="res%d" % c)
-            nc.vector.tensor_tensor(res[:], old_sb[:, :, cols], scaled[c][:], ALU.subtract)
-            nc.sync.dma_start(out_v[:, :, cols], res[:])
+            if c < CHUNKS - 1:
+                nc.vector.tensor_tensor(res[:], old_sb[:, :, cols], scaled[c][:], ALU.subtract)
+                nc.sync.dma_start(out_v[:, :, cols], res[:])
+            else:
+                for r, queue in enumerate((nc.sync, nc.scalar)):
+                    nc.vector.tensor_tensor(res[:, r, :], old_sb[:, r, cols], scaled[c][:, r, :], ALU.subtract)
+                    queue.dma_start(out_v[:, r, cols], res[:, r, :])
 
         stages = (finish, scale_scores, make_ratio, spread, score)
         for step in range(CHUNKS + len(stages) - 1):

from contextlib import ExitStack

import concourse.mybir as mybir

D, T, U, I, J, G = 512, 1024, 1024, 256, 512, 32
FLOPS = 2 * D * I * J

F32 = mybir.dt.float32
BF16 = mybir.dt.bfloat16
I32 = mybir.dt.int32
U32 = mybir.dt.uint32
U16 = mybir.dt.uint16
U8 = mybir.dt.uint8
FP8X4 = mybir.dt.float8_e4m3fn_x4
ACT = mybir.ActivationFunctionType
ALU = mybir.AluOpType
AX = mybir.AxisListType

P = 128
PACK = 4
GROUP = J // G
ROW_TILES = I // P
CHUNK = 128
CHUNKS = J // CHUNK
CG = CHUNK // GROUP
SCALE_ROWS = 16
SCALE_BASE = P - SCALE_ROWS


def tile_attend_bgroupspread_kernel(tc, taba, tabb_words, tabb_scales, aim, old, offs, offs2, out):
    nc = tc.nc
    with ExitStack() as ctx:
        keep = ctx.enter_context(tc.tile_pool(name="keep", bufs=1))
        psum = ctx.enter_context(tc.psum_pool(name="psum", bufs=1))

        list_b = keep.tile([P, J // 16], U16, name="list_b")
        list_a = keep.tile([P, I // 16], U16, name="list_a")
        nc.sync.dma_start(list_b[:], offs2)
        scale_table = keep.tile([P, U], U8, name="scale_table", align_bytes=64)
        nc.scalar.dma_start(scale_table[SCALE_BASE:P, :].bitcast(I32), tabb_scales[0].bitcast(I32))
        nc.sync.dma_start(list_a[:], offs)
        planes_hbm = taba.rearrange("(p t) c -> t p c", t=PACK)
        planes = []
        for t in range(PACK):
            plane = keep.tile([P, T], F32, name="plane%d" % t, tag="plane%d" % t, align_bytes=64)
            nc.scalar.dma_start(plane[:], planes_hbm[t])
            planes.append(plane)

        nc.vector.memset(scale_table[0:SCALE_BASE, :].bitcast(I32), 0)
        b_scales = keep.tile([P, J], U8, name="b_scales", align_bytes=64)
        nc.vector.memset(b_scales[:].bitcast(I32), 0)
        one = keep.tile([P, 1], F32, name="one")
        warm = keep.tile([P, 1], F32, name="warm")
        nc.vector.memset(one[:], 1.0)
        nc.scalar.activation(warm[:], one[:], ACT.Abs_reciprocal_sqrt)

        picked_scales = keep.tile([P, J], U8, name="picked_scales", align_bytes=64)
        nc.vector.tensor_copy(picked_scales[:], scale_table[:].indirect(list_b[:]))
        for q, queue in enumerate((nc.gpsimd, nc.scalar, nc.scalar, nc.scalar)):
            queue.dma_start(b_scales[32 * q:32 * q + 4, :].bitcast(I32),
                              picked_scales[SCALE_BASE + 4 * q:SCALE_BASE + 4 * q + 4, :].bitcast(I32))

        grouped = keep.tile([P, I, PACK], BF16, name="grouped", align_bytes=64)
        for t in range(PACK - 1):
            nc.vector.tensor_copy(grouped[:, :, t], planes[t][:].indirect(list_a[:]))
        word_table = keep.tile([P, U], U32, name="word_table", tag="plane0", align_bytes=64)
        nc.scalar.dma_start(word_table[:].bitcast(I32),
                            tabb_words[0].rearrange("p n t -> p (n t)").bitcast(I32))
        aim_sb = keep.tile([P, ROW_TILES, G], F32, name="aim_sb", tag="plane2", align_bytes=64)
        nc.sync.dma_start(aim_sb[:], aim.rearrange("(t p) g -> p t g", p=P))
        for r in range(ROW_TILES):
            nc.vector.tensor_copy(grouped[:, r * P:(r + 1) * P, PACK - 1],
                                  planes[PACK - 1][:].indirect(list_a[:, 8 * r:8 * r + 8]))
        old_sb = keep.tile([P, ROW_TILES, J], F32, name="old_sb", tag="plane3", align_bytes=64)
        nc.sync.dma_start(old_sb[:], old.rearrange("(t p) j -> p t j", p=P))
        a_codes, a_scales = [], []
        for r in range(ROW_TILES):
            codes = keep.tile([P, P], U32, name="a_codes%d" % r, align_bytes=64)
            scales = keep.tile([P, P], U8, name="a_scales%d" % r, align_bytes=64)
            nc.vector.quantize_mx(out=codes[:].bitcast(FP8X4), scales=scales[:],
                                  in_=grouped[:, r * P:(r + 1) * P, :].rearrange("p c t -> p (c t)"))
            a_codes.append(codes)
            a_scales.append(scales)

        out_v = out.rearrange("(t p) j -> p t j", p=P)
        b_words = []
        for c in range(CHUNKS):
            picked = keep.tile([P, CHUNK], U32, name="b_words%d" % c, align_bytes=64)
            nc.vector.tensor_copy(picked[:], word_table[:].indirect(list_b[:, c * 8:(c + 1) * 8]))
            b_words.append(picked)

        pieces, squares, inv, ratio, scaled = {}, {}, {}, {}, {}

        def score(c):
            cols = slice(c * CHUNK, (c + 1) * CHUNK)
            per_bank = 1 if c < 1 else ROW_TILES
            pieces[c], squares[c] = [], []
            for r0 in range(0, ROW_TILES, per_bank):
                bank = psum.tile([P, per_bank, CHUNK], F32, name="bank%d_%d" % (c, r0))
                for r in range(r0, r0 + per_bank):
                    nc.tensor.matmul_mx(out=bank[:, r - r0, :], lhsT=a_codes[r][:].bitcast(FP8X4),
                                        lhsT_scale=a_scales[r][:], rhs=b_words[c][:].bitcast(FP8X4),
                                        rhs_scale=b_scales[:, cols], start=True, stop=True)
                sq = keep.tile([P, per_bank * CHUNK], F32, name="sq%d_%d" % (c, r0))
                nc.scalar.activation(sq[:], bank[:].rearrange("p t j -> p (t j)"), ACT.Square)
                pieces[c].append((bank, r0, per_bank))
                squares[c].append(sq)

        def spread(c):
            sm = keep.tile([P, ROW_TILES * CG], F32, name="sum%d" % c)
            for (bank, r0, n), sq in zip(pieces[c], squares[c]):
                nc.vector.tensor_reduce(sm[:, r0 * CG:(r0 + n) * CG],
                                        sq[:].rearrange("p (g e) -> p g e", e=GROUP), AX.X, ALU.add)
            inv[c] = keep.tile([P, ROW_TILES * CG], F32, name="inv%d" % c)
            nc.scalar.activation(inv[c][:], sm[:], ACT.Abs_reciprocal_sqrt, bias=0.05, scale=1.0 / GROUP)

        def make_ratio(c):
            ratio[c] = keep.tile([P, ROW_TILES, CG], F32, name="ratio%d" % c)
            nc.vector.tensor_tensor(ratio[c][:], inv[c][:].rearrange("p (t g) -> p t g", g=CG),
                                    aim_sb[:, :, c * CG:(c + 1) * CG], ALU.mult)

        def scale_scores(c):
            scaled[c] = keep.tile([P, ROW_TILES, CHUNK], F32, name="scaled%d" % c)
            for bank, r0, n in pieces[c]:
                nc.vector.scalar_tensor_tensor(
                    scaled[c][:, r0:r0 + n, :].rearrange("p t (g e) -> p (t g) e", e=GROUP),
                    ratio[c][:, r0:r0 + n, :].rearrange("p t g -> p (t g)").unsqueeze(2).to_broadcast([P, n * CG, GROUP]),
                    1.0,
                    bank[:].rearrange("p t (g e) -> p (t g) e", e=GROUP),
                    ALU.subtract, ALU.mult)

        def finish(c):
            cols = slice(c * CHUNK, (c + 1) * CHUNK)
            res = keep.tile([P, ROW_TILES, CHUNK], F32, name="res%d" % c)
            if c < CHUNKS - 1:
                nc.vector.tensor_tensor(res[:], old_sb[:, :, cols], scaled[c][:], ALU.subtract)
                nc.sync.dma_start(out_v[:, :, cols], res[:])
            else:
                for r, queue in enumerate((nc.sync, nc.scalar)):
                    nc.vector.tensor_tensor(res[:, r, :], old_sb[:, r, cols], scaled[c][:, r, :], ALU.subtract)
                    queue.dma_start(out_v[:, r, cols], res[:, r, :])

        stages = (finish, scale_scores, make_ratio, spread, score)
        for step in range(CHUNKS + len(stages) - 1):
            for lag, stage in enumerate(reversed(stages)):
                if 0 <= step - lag < CHUNKS:
                    stage(step - lag)
